import numpy as np, ml_dtypes
CORES = [16,18,20,22]
N = 4
import mx_ref
BF = ml_dtypes.bfloat16
def tile(rs):
    return np.stack(rs, axis=2).reshape(128, -1).astype(BF)
def pick(q, e):
    c = np.concatenate([q[0].reshape(128, -1, 4), np.zeros((128, 1, 4), np.uint8)], axis=1); s = np.concatenate([q[1], np.ones((16, 1), np.uint8)], axis=1)
    return (np.ascontiguousarray(c[:, e].reshape(128, -1)), np.ascontiguousarray(s[:, e]))
def join(*qs):
    return (np.concatenate([q[0] for q in qs], axis=1), np.concatenate([q[1] for q in qs], axis=1))
def put(q, e, v):
    c, s = q[0].reshape(128, -1, 4).copy(), q[1].copy(); c[:, e] = v[0].reshape(128, -1, 4); s[:, e] = v[1]
    return (c.reshape(128, -1), s)
def pk(c, s):
    return (np.ascontiguousarray(c), mx_ref.live(s))
def emit(q):
    return q[0], q[1]
def packed(v, rng):
    q = [mx_ref.quantize(np.ascontiguousarray(v[r])) for r in range(N)]
    return np.stack([a for a, b in q]), np.stack([mx_ref.plane(b, rng) for a, b in q])
def values_of_codes():
    e, c = np.zeros((128, 128, 4), np.float32), np.zeros((128, 2, 4), np.uint8)
    e[np.arange(128), np.arange(128), 0] = 1
    c[:127, :, 0] = np.arange(256).reshape(2, 128).T[:127]
    return mx_ref.matmul(mx_ref.quantize(e.reshape(128, 512).astype(BF)), (c.reshape(128, 8), np.full((16, 2), 127, np.uint8))).T.reshape(-1).astype(np.float64)
CODE_VALUE, SCALE_VALUE = values_of_codes(), 2.0 ** (np.arange(256) - 127.0)
def decode(q):
    return (CODE_VALUE[q[0]].reshape(16, 8, -1, 4) * SCALE_VALUE[q[1]][:, None, :, None] + 0.0).reshape(128, -1).astype(np.float32)
def f(rng, *shape):
    return mx_ref.flush((rng.standard_normal(shape, dtype=np.float32) * np.exp2(rng.integers(-2, 3, shape[:-1] + (1,)))).astype(BF))
def wide(rng, *shape, cols=0):
    v = rng.standard_normal(shape, dtype=np.float32) * np.exp2(rng.integers(-12, 13, shape)).astype(np.float32)
    if cols: v *= np.repeat(np.exp2(rng.integers(-cols, cols + 1, shape[:-2] + (1, shape[-1] // 4))) * (rng.random(shape[:-2] + (1, shape[-1] // 4)) > 0.0625), 4, axis=-1).astype(np.float32)
    return mx_ref.flush(v.astype(BF))
C, H = 320, 96
DIST = [1, 2, 3]
def numbers_of(rng):
    return {"x": np.array(f(rng, N, 128, 4 * C)), "u": np.array(f(rng, N, 128, 512)), "v": np.array(f(rng, N, 128, 512))}
def changes(rng):
    return np.argsort(rng.random((N, 8, 8)), axis=2).astype(np.int32)
def layers(rng, still=[]):
    k = np.exp2(np.argsort(rng.random((N, 128, 1)), axis=1) % 5 - 6.0).astype(np.float32)
    w = np.array(mx_ref.flush((rng.standard_normal((N, 128, 2048), dtype=np.float32) * k).astype(BF))).reshape(N, 8, 16, 4, 8, 16, 4)
    for i in still:
        w[:, :, i] = 0
        w[:, :, :, :, :, i] = 0
    return w
def weights(rng, w):
    c, p = packed(np.ascontiguousarray(w).reshape(N, 128, 2048), rng)
    return {"wc": c, "ws": p}
def edges(rng, x):
    x = x.astype(np.float32).reshape(N, 8, 16, C, 4)
    k = (N, 8, 8, C, 4)
    a = (2 * rng.integers(64, 128, k) + 1) * np.exp2(-7.0 - rng.integers(8, 15, k)) * (rng.integers(0, 2, k) * 2.0 - 1.0)
    a[:, :, 0, :, 0] = 1.96875
    x[:, :, 8:] = a * np.exp2(rng.integers(-2, 3, (N, 8, 1, C, 1)))
    return x
def undecided(u):
    u = u.reshape(N, 128, 128, 4)
    u[:, :, ::16] = 0
    u[:, :, 1:4] = 0
    return u
def setup_inputs(rng):
    return {**numbers_of(rng), "ch": changes(rng), **weights(rng, layers(rng))}
def setup_inputs_ties(rng):
    d = numbers_of(rng)
    x = edges(rng, d["x"])
    k = rng.integers(-1, 2, (N, 8, C)).astype(np.float32)
    o = rng.permutation(N)
    k[o[0]] = 0
    k[o[1]] = rng.integers(0, 2, (8, 1)) * 2.0 - 1.0
    x[:, :, 0] = 0
    x[:, :, 0, :, 0] = k
    u = undecided(d["u"])
    for h in range(0, 128, 16): u[:, h, h, 0] = 1.0
    for b in range(3): u[:, 16 * b, 1 + b, 0] = 1.0
    return {"x": x.reshape(N, 128, 4 * C).astype(BF), "u": u.reshape(N, 128, 512), "v": d["v"], "ch": changes(rng), **weights(rng, layers(rng, [0]))}
def setup_inputs_near(rng):
    d = numbers_of(rng)
    x = d["x"].astype(np.float32).reshape(N, 8, 16, C, 4)
    s = rng.integers(0, 256, (N, 8, C))
    x[:, :, 0] = 0
    x[:, :, 8:] = 0
    x[:, :, 0, :, 0] = rng.integers(0, 2, (N, 8, C)) * 2.0 - 1.0
    for i in range(2): x[:, :, 8 + i] = ((s[:, :, :, None] >> (4 * i + np.arange(4))) & 1) * np.exp2(4.0 * i + np.arange(4) - 23.0)
    x[:, :, 11, :, 0] = 2.0 ** -10
    x[:, :, 12, :, :3] = rng.integers(-1, 2, (N, 8, C, 3)) * 2.0 ** -22
    o = rng.permutation(N) % 4
    x[o == 3, :, 8:] *= np.float32(2.0 ** -7)
    x[o == 3, :, 12:13] *= np.float32(0.5)
    u = undecided(d["u"])
    for r in range(N):
        k = 1.0 if o[r] == 0 else 2.0 ** -30
        for h in range(0, 128, 16):
            u[r, h + 8:h + 10, h] = k
            if o[r] < 2:
                u[r, h, h, 0] = k
                u[r, h + 11, h, 0] = k
        for b in range(3): u[r, 16 * b + 12, 1 + b, b] = k
    return {"x": x.reshape(N, 128, 4 * C).astype(BF), "u": u.reshape(N, 128, 512), "v": d["v"], "ch": changes(rng), **weights(rng, layers(rng, [0, 8, 9, 10, 11, 12, 13, 14, 15]))}
def setup_inputs_calls(rng):
    d = numbers_of(rng)
    x = edges(rng, d["x"])
    x[:, :, 0] = (-(1.0 + 0.125 * rng.permutation(N)) * 2.0 ** -6)[:, None, None, None]
    o = rng.permutation(N) % 2 * 2.0 - 1.0
    u = d["u"].reshape(N, 128, 128, 4)
    u[:, :, 1:4] = 0
    for r in range(N):
        for b in range(3): u[r, 16 * b, 1 + b, b] = float(o[r])
    return {"x": x.reshape(N, 128, 4 * C).astype(BF), "u": u.reshape(N, 128, 512), "v": d["v"], "ch": changes(rng), **weights(rng, layers(rng))}
def setup_inputs_ends(rng):
    d = numbers_of(rng)
    o = np.array([0, 2, 3, 1])[(np.arange(N) + rng.integers(4)) % 4]
    x = 2.0 ** 25 * (1.0 - 0.125 * rng.integers(0, 3, (N, 8, 16, C, 4)))
    x = np.where((o < 2)[:, None, None, None, None], x, 2.0 ** -30 * (1.0 + 0.125 * rng.integers(0, 8, (N, 1, 1, C, 1))))
    x[o == 1] *= rng.integers(0, 2, (1, 1, 1, C, 1)) * 2.0 - 1.0
    u = d["u"].astype(np.float32).reshape(N, 128, 128, 4)
    v = np.zeros((N, 128, 512), np.float32)
    w = np.zeros((N, 128, 4, 128, 4), np.float32)
    i, e = np.arange(128), np.arange(8)
    for r in range(N):
        a = 2.0 ** 30 if o[r] < 2 else 2.0 ** -30
        k = np.full((128, 8, 4), a)
        if o[r] < 2: k *= 1.0 - 0.125 * rng.integers(0, 3, (128, 8, 4))
        t = np.ones(8) if o[r] == 2 else rng.permutation(8) % 2 * 2.0 - 1.0
        u[r][:, ::16] = k * t[None, :, None]
        if o[r] > 1: u[r][:, 16 * rng.permutation(8)[:2]] = 0
        u[r][:, 1:4] = -a if o[r] == 3 else a
        v[r] = a * (rng.integers(0, 2, (128, 512)) * 2.0 - 1.0)
        if o[r] % 2 == 0: w[r] = 0.125
        else:
            for b in range(4): w[r, i, b, i, b] = 64.0 if o[r] == 1 else 2.0 ** -30
    ch = changes(rng)
    ch[o == 0] = (e + 1) % 8
    ch[o == 1] = e
    ch[o == 2] = 7 - e
    return {"x": x.astype(np.float32).reshape(N, 128, 4 * C).astype(BF), "u": u.reshape(N, 128, 512).astype(BF), "v": v.astype(BF), "ch": ch, **weights(rng, w.astype(BF))}
def setup_inputs_spread(rng):
    d = setup_inputs(rng)
    d["x"] = wide(rng, N, 128, 4 * C, cols=6)
    return d
def check_inputs(d):
    b = []
    for k, most in (("x", 2.0 ** 25), ("u", 2.0 ** 30), ("v", 2.0 ** 30)):
        a = np.abs(d[k].astype(np.float32))
        if not (np.isfinite(a).all() and ((a == 0) | (a >= 2.0 ** -30) & (a <= most)).all()): b.append("a value of " + k)
    if not (np.sort(d["ch"], axis=2) == np.arange(8)).all(): b.append("a row of ch")
    none, least, most = [emit(mx_ref.quantize(np.full((128, 16), k, np.float32).astype(BF)))[1][0, 0] for k in (0.0, 2.0 ** -30, 2.0 ** 30)]
    for r in range(N):
        if ((d["wc"][r] == 0x7F) | (d["wc"][r] == 0xFF)).any(): b.append("wc: a code that is no number")
        s = mx_ref.live(d["ws"][r])
        if ((s != none) & ((s < least) | (s > most))).any(): b.append("ws: a scale out of range")
        a = np.abs(decode(pk(d["wc"][r], d["ws"][r])).astype(np.float64)).reshape(128, 512, 4)
        if not (np.sum(a, axis=(0, 2)) <= 64).all(): b.append("sizes in a column of W")
    return b
def reference(x, u, v, ch, wc, ws):
    qu = [mx_ref.quantize(u[r]) for r in range(N)]
    lay = [pk(wc[r], ws[r]) for r in range(N)]
    now = [x[r] for r in range(N)]
    last = [None] * N
    for d in DIST:
        rung = []
        for r in range(N):
            q = mx_ref.quantize(now[r])
            s = mx_ref.matmul(qu[r], q) + np.float32(0.0)
            order = np.argsort(-s[::16], axis=1, kind="stable")
            a = ch[r][4 * (s[1] > 0) + 2 * (s[2] > 0) + (s[3] > 0)]
            row = np.array(a)
            for j in range(1, C): row[j] = row[j - 1][a[j]]
            h = np.ascontiguousarray(row.T)
            c = np.take_along_axis(order, h, axis=0)
            parts = decode(q).astype(BF).reshape(8, 16, C, 4)
            rung.append(np.ascontiguousarray(parts[h, :, c].transpose(0, 2, 1, 3)).reshape(128, 4 * C))
            last[r] = h
        sent = [mx_ref.quantize(np.ascontiguousarray(rung[r][:, :4 * H])) for r in range(N)]
        for r in range(N):
            came = sent[(r - d) % N]
            own = decode(came)
            first = tile([np.maximum(mx_ref.matmul(pick(lay[r], np.arange(128 * b, 128 * b + 128)), came), np.float32(0.0)) * np.float32(0.03125) + own[:, b::4] for b in range(4)])
            now[r] = np.concatenate([first, rung[r][:, 4 * H:]], axis=1)
    y, rw = np.zeros((N, 128, C), np.float32), np.zeros((N, 8, C), np.float32)
    oc, osc = np.zeros((N, 128, 4 * C), np.uint8), np.zeros((N, 16, C), np.uint8)
    for r in range(N):
        q = mx_ref.quantize(now[r])
        y[r] = mx_ref.matmul(mx_ref.quantize(v[r]), q)
        rw[r] = last[r]
        oc[r], osc[r] = emit(q)
    return {"y": y, "rw": rw, "oc": oc, "osc": osc}

@@ -1,0 +1,676 @@
+from concourse.mybir import dt, AluOpType, ActivationFunctionType
+
+STEP = 16384.0
+LOW = 4194304.0
+SLACK = 60.0
+CY = 0.83
+CHAIN = {"o": "s", "n": "x"}
+ROUNDS = 3
+NP = {"o": 224, "n": 96}
+ST = {"o": 8, "n": 4}
+F32, BF, I32, U16 = "float32", "bfloat16", "int32", "uint16"
+CODE, SC = "float8_e4m3fn_x4", "uint8"
+
+
+def _scratch():
+    d = {}
+
+    def sb(name, n, t=F32):
+        d[name] = ("sbuf", [128, n], t)
+
+    def mx(name, n):
+        sb(name + "c", n, CODE)
+        sb(name + "s", n, SC)
+    for b in range(8):
+        d["ps%d" % b] = ("psum", [128, 512], F32)
+    for n, w in (("xb", 1280), ("ub", 512), ("vb", 512), ("eb", 2048), ("mvb", 1536), ("zb", 512), ("ccb", 1024), ("xnb", 512), ("tb", 1280),
+                 ("win", 10240), ("sto", 1024), ("stn", 512), ("mao", 128), ("man", 128), ("mb", 128), ("go", 3584), ("gn", 2560), ("jk", 1280)):
+        sb(n, w, BF)
+    for n, w in (("uq", 128), ("ur", 128), ("vq", 128), ("eq", 512), ("mv", 384), ("zq", 128), ("wq", 512), ("cc", 256), ("sqo", 256), ("sqn", 128),
+                 ("gq", 896), ("gw", 448)):
+        mx(n, w)
+    for r in range(ROUNDS + 1):
+        mx("qt%d" % r, 320)
+        if r:
+            mx("ld%d" % r, 128)
+            mx("xn%d" % r, 128)
+    for n in ("pi", "gi", "ii", "e1", "e2", "e3", "e4", "i7i"):
+        sb(n, 1, I32)
+    for n in ("m16", "mk", "ml", "mg", "dr", "dl", "sd", "ob", "ol", "row", "rol", "os1", "os2", "yb", "rwa", "rwb"):
+        sb(n, 320)
+    for n in ("chf", "m8", "k8", "d8", "cht", "chs", "t1"):
+        sb(n, 64)
+    for n, w in (("cf", 48), ("rl", 384), ("bt0", 3), ("bt1", 3), ("cn", 20), ("nn", 128), ("m64", 512), ("ones", 128), ("eye", 128), ("ulf", 8),
+                 ("clo", 8), ("chh", 8), ("rr", 224), ("rv", 224), ("acl", 6), ("aft", 14), ("cs", 14), ("rkc", 14), ("rko", 14), ("cl", 224),
+                 ("ow", 160), ("rxf", 20), ("r64", 20), ("fo", 20)):
+        sb(n, w)
+    sb("chi", 64, I32), sb("chb", 64, I32), sb("rwi", 320, I32)
+    for n, w in (("ul", 8), ("rlst", 14), ("rk16", 20), ("rx", 20), ("fl0", 20), ("fl1", 20), ("fl2", 20), ("fl3", 20)):
+        sb(n, w, U16)
+    for p, n in NP.items():
+        S, nc, st = n // 16, n // 32, ST[p]
+        for k, w in (("id", 16 * nc), ("xw", 256 * nc), ("tw", 16 * nc), ("tv", nc), ("lf", 16 * st), ("ac", 16 * st), ("ta", 16 * S + 16), ("cb", nc),
+                     ("f1f", S), ("lr", n), ("lw", n), ("zz", 224 if p == "o" else 192), ("ab", n), ("am", n), ("sx", n), ("so", n), ("sg", n)):
+            sb(k + p, w)
+        for k, w in (("ix", st), ("li", 16 * st), ("tl", 2 * nc), ("f1", S), ("ll", S)):
+            sb(k + p, w, U16)
+    return d
+
+
+def _pack(d):
+    place, at, rest = {}, {}, {}
+    for name, (where, shape, t) in d.items():
+        host = {F32: "kf", U16: "ku", I32: "ki"}.get(t)
+        if where != "sbuf" or host is None or name in ("chi", "ow", "yb", "rwb"):
+            rest[name] = (where, shape, t)
+            continue
+        place[name] = (host, at.get(host, 0))
+        at[host] = at.get(host, 0) + (shape[1] + 15) // 16 * 16
+    for host, t in (("kf", F32), ("ku", U16), ("ki", I32)):
+        rest[host] = ("sbuf", [128, at[host]], t)
+    return rest, place
+
+
+BUFS = _scratch()
+SCRATCH, PLACE = _pack(BUFS)
+SEMAPHORES = (["cv", "ct", "cs", "cg", "dx", "du", "dv", "dw", "dc", "zf", "out", "ls"]
+              + [k + "%d" % r for k in ("fo", "fn", "od") for r in range(3)] + ["rc%d" % r for r in range(1, 4)])
+
+
+def _make(g, T):
+    queues = {"v": g.vector, "t": g.tensor, "s": g.scalar, "g": g, "y": g.sync}
+    comp = {"v": "cv", "t": "ct", "s": "cs", "g": "cg"}
+    total, known, recs, jobs = {}, {q: {} for q in queues}, {}, []
+
+    def view(a):
+        n, lo, hi, st = a
+        return T[n][:, lo:hi] if st == 1 else T[n][:, lo:hi:st]
+
+    def span(a):
+        return (a[0], 0, 512, 1, True) if a[0][:2] == "ps" else (a[0], a[1], a[2], a[3], False)
+
+    def meet(lo, hi, st, x):
+        return x[0] < hi and lo < x[1] and not (st == x[2] and st > 1 and (lo - x[0]) % st)
+
+    def cover(lo, hi, st, x):
+        return lo <= x[0] and x[1] <= hi and (st == 1 or (st == x[2] and (lo - x[0]) % st == 0))
+
+    def wait(q, sem, val, clk):
+        k = known[q]
+        if k.get(sem, 0) >= val:
+            return
+        queues[q].wait_ge(T.sem[sem], int(val))
+        k[sem] = val
+        for s, x in clk.items():
+            if k.get(s, 0) < x:
+                k[s] = x
+
+    def need(q, reads, writes, sem, self_ok):
+        deps = []
+        for lst, isw in ((reads, False), (writes, True)):
+            for a in lst:
+                n, lo, hi, st, ps = span(a)
+                for x in recs.get(n, []):
+                    rw, rq, rsem = x[3], x[4], x[5]
+                    if not meet(lo, hi, st, x) or not (isw or rw or (ps and rq != q)):
+                        continue
+                    if rq == q == "t" and rw and isw:
+                        continue
+                    if rsem == sem and not self_ok:
+                        continue
+                    deps.append((rsem, x[6], x[7]))
+        deps.sort(key=lambda d: -sum(d[2].values()))
+        for s, v, c in deps:
+            wait(q, s, v if s in comp.values() else total[s], c)
+
+    def note(q, reads, writes, sem, val):
+        clk = dict(known[q])
+        for lst, isw in ((reads, False), (writes, True)):
+            for a in lst:
+                n, lo, hi, st, ps = span(a)
+                old = recs.get(n, [])
+                if isw:
+                    old = [x for x in old if not cover(lo, hi, st, x) or (x[5] == sem and sem not in comp.values())]
+                else:
+                    old = [x for x in old if not (not x[3] and x[4] == q and x[5] == sem and cover(lo, hi, st, x))]
+                recs[n] = old + [(lo, hi, st, isw, q, sem, val, clk)]
+
+    def put(q, reads, writes, fn):
+        sem = comp[q]
+        need(q, reads, writes, sem, True)
+        total[sem] = total.get(sem, 0) + 1
+        fn(queues[q]).then_inc(T.sem[sem], 1)
+        note(q, reads, writes, sem, total[sem])
+
+    def put_dma(q, sem, reads, writes, out, in_):
+        need(q, reads, writes, sem, False)
+        total[sem] = total.get(sem, 0) + 16
+        queues[q].dma_start(out, in_).then_inc(T.sem[sem], 16)
+        note(q, reads, writes, sem, total[sem])
+
+    def op(q, reads, writes, fn, cost=60.0):
+        jobs.append(dict(q=q, r=reads, w=writes, fn=fn, cost=cost, lat=0.0, sem=None))
+
+    def dma(q, sem, reads, writes, out, in_, lat=2000.0):
+        jobs.append(dict(q=q, r=reads, w=writes, fn=(out, in_), cost=60.0, lat=lat, sem=sem))
+
+    def raw(q, reads, writes, fn, cost, lat):
+        jobs.append(dict(q=q, r=reads, w=writes, fn=fn, cost=cost, lat=lat, sem="raw"))
+
+    def run():
+        table, groups, n = {}, {}, len(jobs)
+        for i, j in enumerate(jobs):
+            pre = set()
+            grp = j["sem"] if j["sem"] not in (None, "raw") else None
+            acc = [(span(a), False) for a in j["r"]] + [(span(a), True) for a in j["w"]]
+            for (nm, lo, hi, st, ps), isw in acc:
+                for x in table.get(nm, []):
+                    k = x[4]
+                    if k != i and meet(lo, hi, st, x) and (x[3] or isw or ps) and (grp is None or jobs[k]["sem"] != grp):
+                        pre.add(k)
+            for (nm, lo, hi, st, ps), isw in acc:
+                old = table.get(nm, [])
+                if isw and grp is None:
+                    old = [x for x in old if not cover(lo, hi, st, x)]
+                table[nm] = old + [(lo, hi, st, isw, i)]
+            for k in list(pre):
+                if jobs[k]["sem"] not in (None, "raw"):
+                    pre.update(groups[jobs[k]["sem"]])
+            pre.discard(i)
+            j["pre"] = pre
+            if grp:
+                groups.setdefault(grp, []).append(i)
+        after = [[] for _ in jobs]
+        for i, j in enumerate(jobs):
+            for k in j["pre"]:
+                after[k].append(i)
+        way = [0.0] * n
+        for i in range(n - 1, -1, -1):
+            way[i] = jobs[i]["cost"] + jobs[i]["lat"] + max([way[k] + 50.0 for k in after[i]] or [0.0])
+        free = {q: 0.0 for q in queues}
+        fin, qof, left = {}, {}, [len(j["pre"]) for j in jobs]
+        ready = [i for i in range(n) if not left[i]]
+        while ready:
+            best = None
+            for i in ready:
+                for q in (("v", "s") if jobs[i]["q"] == "x" else (jobs[i]["q"],)):
+                    t = 0.0
+                    for k in jobs[i]["pre"]:
+                        t = max(t, fin[k] + (25.0 if qof[k] == q else 70.0))
+                    key = (max(free[q], t - SLACK), -way[i], max(free[q], t))
+                    if best is None or key < best[0]:
+                        best = (key, i, q)
+            key, i, q = best
+            j = jobs[i]
+            ready.remove(i)
+            free[q] = key[2] + j["cost"]
+            fin[i] = free[q] + j["lat"]
+            qof[i] = q
+            if j["sem"] is None:
+                put(q, j["r"], j["w"], j["fn"])
+            elif j["sem"] == "raw":
+                j["fn"]()
+            else:
+                put_dma(q, j["sem"], j["r"], j["w"], j["fn"][0], j["fn"][1])
+            for k in after[i]:
+                left[k] -= 1
+                if not left[k]:
+                    ready.append(k)
+        jobs.clear()
+    return dict(view=view, wait=wait, need=need, op=op, dma=dma, raw=raw, run=run, total=total)
+
+
+def rank_program(g, core, T, topo):
+    rank = T.rank_of(core)
+    if rank is None:
+        return
+    K = _make(g, T)
+    view, op, dma, raw = K["view"], K["op"], K["dma"], K["raw"]
+    A, ACT = AluOpType, ActivationFunctionType
+
+    def B(n, lo=0, hi=None, st=1):
+        h, at = PLACE.get(n, (n, 0))
+        return (h, at + lo, at + (BUFS[n][1][1] if hi is None else hi), st)
+
+    def cf(j):
+        return B("cf", j, j + 1)
+
+    def ps(b, lo, hi):
+        return ("ps%d" % b, lo, hi, 1)
+
+    def width(a):
+        return (a[2] - a[1] + a[3] - 1) // a[3]
+
+    def small(a):
+        return SCRATCH[a[0]][2] in (BF, U16)
+
+    def vc(out, ins, two=False):
+        n = width(out)
+        if any(a[0] == "@" for a in ins):
+            return 50 + 1.5 * CY * n
+        if two and not any(a[0][:2] == "ps" for a in ins):
+            return max(64, 2 * n) * CY
+        return max(64, n * (0.5 if small(out) and all(small(a) for a in ins) else 1.0)) * CY
+
+    def acost(out, ins):
+        return (65 + 1.5 * CY * width(out)) if any(a[0] == "@" for a in ins) else 50 + CY * width(out)
+
+    def sc(x):
+        return (view(x), [x]) if isinstance(x, tuple) else (x, [])
+
+    def src(a):
+        if a[0] == "@":
+            return view(a[1]).indirect(view(a[2])), [a[1], a[2]]
+        return view(a), [a]
+
+    def ts(out, in0, s1, op0, s2=None, op1=None):
+        iv, ir = src(in0)
+        (x1, r1), (x2, r2) = sc(s1), sc(s2)
+
+        def vec(e):
+            if op1 is None:
+                return e.tensor_scalar(view(out), iv, x1, None, op0)
+            return e.tensor_scalar(view(out), iv, x1, x2, op0, op1)
+
+        def either(e):
+            if e is g.vector:
+                return vec(e)
+            m, a = (x1, 0.0 if op1 is None else x2) if op0 == A.mult else (1.0, x1)
+            return e.activation(view(out), iv, ACT.Identity, bias=a, scale=m)
+        plain = SCRATCH[out[0]][2] == F32 and SCRATCH[in0[0]][2] == F32 and (op0 == A.mult and op1 in (None, A.add) or op0 == A.add and op1 is None)
+        if plain:
+            op("x", ir + r1 + r2, [out], either, 10 + vc(out, [in0]))
+        else:
+            op("v", ir + r1 + r2, [out], vec, vc(out, [in0]))
+
+    def tt(out, in0, in1, o):
+        iv, ir = src(in0)
+        op("v", ir + [in1], [out], lambda e: e.tensor_tensor(view(out), iv, view(in1), o), vc(out, [in0, in1], True))
+
+    def cp(out, in_, q="v"):
+        iv, ir = src(in_)
+
+        def fn(e):
+            if e is g.vector:
+                return e.tensor_copy(view(out), iv)
+            return e.activation(view(out), iv, ACT.Copy)
+        op(q, ir, [out], fn, vc(out, [in_]) if q == "v" else acost(out, [in_]))
+
+    def lay(out, in_, col):
+        def fn(e):
+            if e is g.vector:
+                return e.tensor_scalar(view(out), view(in_), view(col), None, A.mult)
+            return e.activation(view(out), view(in_), ACT.Copy, scale=view(col))
+        op("x", [in_, col], [out], fn, 90.0)
+
+    def scan(out, d0, d1, o0, o1):
+        op("v", [d0, d1], [out], lambda e: e.tensor_tensor_scan(view(out), view(d0), view(d1), 0.0, o0, o1), CY * width(out))
+
+    def latch(out, d1):
+        scan(out, B("dl", 0, width(d1)), d1, A.add, A.max)
+
+    def fill(out, x):
+        op("v", [], [out], lambda e: e.memset(view(out), x), vc(out, []))
+
+    def iota(out, pat, base=0, cm=0):
+        if SCRATCH[out[0]][2] == I32:
+            op("g", [], [out], lambda e: e.iota(view(out), pat, base, cm), 150.0)
+        else:
+            op("g", [], [out], lambda e: e.iota(view(out), pat, base, cm, allow_small_or_imprecise_dtypes=True), 130 + 2 * CY * width(out))
+
+    def quant(name, lo, hi, tile, tlo):
+        t = (tile, tlo, tlo + 4 * (hi - lo), 1)
+        c, s = (name + "c", lo, hi, 1), (name + "s", lo, hi, 1)
+        op("v", [t], [c, s], lambda e: e.quantize_mx(view(c), view(s), view(t)), 12 + 0.88 * (hi - lo))
+
+    def mm(bank, n, w, wlo, x, xlo, start=True, stop=True):
+        lc, ls = (w + "c", wlo, wlo + 128, 1), (w + "s", wlo, wlo + 128, 1)
+        rc, rs = (x + "c", xlo, xlo + n, 1), (x + "s", xlo, xlo + n, 1)
+        o = ps(bank, 0, n)
+        op("t", [lc, ls, rc, rs], [o], lambda e: e.matmul_mx(view(o), view(lc), view(ls), view(rc), view(rs), start, stop), 0.6 * (n + 16))
+
+    dma("y", "dx", [], [B("xb")], view(B("xb")), T.x[:, :])
+    dma("s", "du", [], [B("ub")], view(B("ub")), T.u[:, :])
+    dma("y", "dc", [], [B("chi")], T.chi[0:1, 0:64], T.ch[:, :])
+    dma("y", "dv", [], [B("vb")], view(B("vb")), T.v[:, :])
+    dma("y", "dw", [], [B("wqc")], T.wqc[:, 0:512].bitcast(dt.uint8), T.wc[:, :])
+    dma("y", "dw", [], [B("wqs")], view(B("wqs")), T.ws[:, :])
+
+    iota(B("pi"), [[1, 1]], 0, 1)
+    iota(B("ulf"), [[16, 8]])
+    iota(B("m16"), [[0, 20], [1, 16]])
+    iota(B("nn"), [[1, 128]])
+    fill(B("eb"), 0.0)
+    fill(B("ones"), 1.0)
+    op("g", [B("ones")], [B("eye")], lambda e: e.affine_select(view(B("eye")), view(B("ones")), [[-1, 128]], A.is_equal, 0.0, 0, 1), 400.0)
+    cp(B("ul"), B("ulf"))
+    quant("uq", 0, 128, "ub", 0)
+    quant("qt0", 0, 320, "xb", 0)
+    op("v", [B("uqc"), B("ul")], [B("urc")], lambda e: e.tensor_copy(T.urc[:, 0:128].bitcast(dt.uint32), T.uqc[:, 0:128].bitcast(dt.uint32).indirect(view(B("ul")))), 210.0)
+    op("v", [B("uqs"), B("ul")], [B("urs")], lambda e: e.tensor_copy(T.urs[:, 0:128], T.uqs[:, 0:128].indirect(view(B("ul")))), 210.0)
+    for b in range(4):
+        cp(B("eb", 512 * b + b, 512 * (b + 1), 4), B("eye"), "x")
+    quant("eq", 0, 512, "eb", 0)
+    ts(B("gi"), B("pi"), 4, A.arith_shift_right)
+    ts(B("ii"), B("pi"), 15, A.bitwise_and)
+    ts(B("e1"), B("ii"), 1, A.bitwise_and)
+    ts(B("e2"), B("ii"), 3, A.bitwise_and)
+    ts(B("e3"), B("ii"), 1, A.arith_shift_right)
+    ts(B("e4"), B("ii"), 2, A.arith_shift_right)
+    ts(B("i7i"), B("ii"), 7, A.bitwise_and)
+    G_, I_, E1, E2, E3, E4, I7, CORR, NCORR, H8, H88 = (cf(j) for j in range(11))
+    for j, n in enumerate(("gi", "ii", "e1", "e2", "e3", "e4", "i7i")):
+        cp(cf(j), B(n))
+    ts(CORR, I_, -STEP, A.mult, 15.0 * STEP, A.add)
+    ts(NCORR, CORR, -1.0, A.mult)
+    ts(H8, I_, 8.0, A.is_ge)
+    ts(H88, H8, 8.0, A.mult)
+    ts(B("mk"), B("m16"), I_, A.is_equal)
+    ts(B("ml"), B("m16"), I_, A.is_lt)
+    ts(B("mg"), B("m16"), I_, A.is_gt)
+    ts(B("dr"), B("m16"), 0.0, A.is_gt)
+    t0, t1, t2, t3, t4, t5, RN, RA, RB, FN, FA = (cf(j) for j in range(11, 22))
+    ts(t0, G_, 3.0, A.is_ge)
+    ts(FN, t0, -7.0, A.mult, 8.0, A.add)
+    ts(t0, t0, -3.0, A.mult, G_, A.add)
+    ts(t1, E2, 4.0, A.mult, t0, A.add)
+    ts(t2, G_, 6.0, A.is_ge, 100.0, A.mult)
+    tt(RN, t1, t2, A.add)
+    ts(t3, G_, 7.0, A.is_ge)
+    ts(FA, t3, -7.0, A.mult, 8.0, A.add)
+    ts(t3, t3, -7.0, A.mult, G_, A.add)
+    ts(RA, E1, 8.0, A.mult, t3, A.add)
+    ts(t4, E1, 8.0, A.mult, G_, A.add)
+    ts(t5, G_, 2.0, A.is_lt, 100.0, A.mult)
+    ts(t4, t4, -1.0, A.add)
+    tt(RB, t4, t5, A.add)
+    for n, r in (("mao", RA), ("mb", RB), ("man", RN)):
+        ts(B(n), B("m16", 0, 128), r, A.is_equal)
+    fill(B("mvb"), 0.0)
+    fill(B("sto"), 0.0)
+    fill(B("stn"), 0.0)
+    for t, w in enumerate((4.0, 2.0, 1.0)):
+        ts(cf(22 + t), FN, w, A.mult)
+        ts(cf(25 + t), FA, w, A.mult)
+        ts(B("mvb", t, 512, 4), B("nn"), E3, A.is_equal, cf(25 + t), A.mult)
+        ts(B("mvb", 512 + t, 1024, 4), B("nn"), E4, A.is_equal, cf(22 + t), A.mult)
+        ts(B("mvb", 1024 + t, 1536, 4), B("nn"), E3, A.is_equal, w, A.mult)
+    quant("mv", 0, 384, "mvb", 0)
+    ts(B("dl"), B("m16"), I_, A.is_gt, LOW + STEP, A.mult)
+    ts(B("dl"), B("dl"), -LOW, A.add)
+    iota(B("m64"), [[1, 8], [0, 64]])
+    ts(B("ccb", 0, 512), B("m64"), G_, A.is_equal)
+    ts(B("ccb", 512, 1024), B("m64"), G_, A.is_equal, -1.0, A.mult)
+    quant("cc", 0, 256, "ccb", 0)
+    fill(B("zb"), 0.0)
+    for q in range(4):
+        fill(B("go", 896 * q + 4 * min(64 * q, 96), 896 * q + 4 * min(64 * q + 64, 224)), 0.0)
+        if q:
+            quant("gq", 224 * q, 224 * q + 128, "zb", 0)
+    fill(B("gn", 1280, 2560), 0.0)
+    fill(B("aft"), 0.0)
+    iota(B("cs"), [[16, 14]], -304)
+    ts(B("cs"), B("cs"), CORR, A.add)
+    op("g", [B("chi")], [B("chb")], lambda e: e.partition_broadcast(view(B("chb")), T.chi[0:1, 0:64], 128), 350.0)
+    iota(B("m8"), [[0, 8], [1, 8]])
+    cp(B("chf"), B("chb"))
+    ts(B("k8"), B("m8"), I7, A.is_equal)
+    ts(B("d8"), B("m8"), 0.0, A.is_gt)
+    tt(B("cht"), B("chf"), B("k8"), A.mult)
+    scan(B("chs"), B("d8"), B("cht"), A.mult, A.add)
+    CHV = B("chs", 7, 64, 8)
+    ts(B("chh"), CHV, H8, A.mult)
+    tt(B("clo"), CHV, B("chh"), A.subtract)
+    for a in range(8):
+        ts(B("t1", 8 * a, 8 * a + 8), B("chh"), B("clo", a, a + 1), A.add)
+    iota(B("tao", 0, 16), [[0, 2], [1, 8]])
+    for p in NP:
+        nc, j = NP[p] // 32, 28 + 3 * "on".index(p)
+        iota(B("id" + p), [[16, nc], [16 * nc + 8, 2], [1, 8]])
+        iota(B("id" + p, 8, 16), [[1, 8]], 16 * nc)
+        iota(B("ac" + p), [[0, 16], [16, ST[p]]])
+        ts(B("ac" + p), B("ac" + p), H88, A.add)
+        iota(B("f1f" + p), [[8, 2], [16, nc]])
+        ts(cf(j), I_, 16.0 * nc, A.mult, G_, A.add)
+        ts(B("f1" + p), B("f1f" + p), cf(j), A.add)
+        iota(B("cb" + p), [[16, nc]])
+        ts(cf(j + 1), H8, 16.0 * nc + 8, A.mult, CORR, A.add)
+        ts(cf(j + 2), H8, 16.0 * nc, A.mult, CORR, A.add)
+        ts(B("cb" + p, 1, nc), B("cb" + p, 1, nc), cf(j + 1), A.add)
+        ts(B("cb" + p, 0, 1), B("cb" + p, 0, 1), cf(j + 2), A.add)
+    TI = B("tan", 0, 16)
+    iota(TI, [[0, 2], [1, 8]])
+    ts(TI, TI, G_, A.subtract)
+    ts(B("rxf", 0, 16), TI, 0.0, A.is_lt, 8.0, A.mult)
+    tt(TI, TI, B("rxf", 0, 16), A.add)
+    ts(TI, TI, 20.0, A.mult)
+    iota(B("sd"), [[4, 320]])
+    ts(B("sd"), B("sd"), NCORR, A.add)
+    iota(B("cn"), [[-1, 20]])
+    ts(B("cn"), B("cn"), CORR, A.add)
+    fill(B("xnb"), 0.0)
+    quant("zq", 0, 128, "zb", 0)
+    for r in range(1, ROUNDS + 1):
+        dma("y", "zf", [B("zqc", 0, 32)], [B("ld%dc" % r, 96, 128)], T["ld%dc" % r][:, 96:128].bitcast(dt.uint8), T.zqc[:, 0:32].bitcast(dt.uint8))
+        dma("y", "zf", [B("zqs", 0, 32)], [B("ld%ds" % r, 96, 128)], T["ld%ds" % r][:, 96:128], T.zqs[:, 0:32])
+    quant("vq", 0, 128, "vb", 0)
+
+    def products(p, x, xlo):
+        n = 224 if p == "o" else 128
+        mm(0, n, "ur", 0, x, xlo)
+        mm(1, n, "ur", 0, x, xlo)
+        mm(2, 128, x, xlo, "uq", 0)
+        if p == "o":
+            mm(7, 128, x, xlo + 96, "uq", 0)
+
+    def calls(p):
+        s = "st" + p
+        for b, m, o in [(2, "ma" + p, 0)] + ([(7, "mb", 512)] if p == "o" else []):
+            bits = "bt%d" % (o // 512)
+            ts(B(bits), ps(b, 1, 4), 0.0, A.is_gt)
+            for t in range(3):
+                lay(B(s, o + t, o + 512, 4), B(m), B(bits, t, t + 1))
+        if p == "o":
+            quant("sqo", 0, 256, s, 0)
+            mm(2, 128, "sqo", 0, "mv", 0, True, False)
+            mm(2, 128, "sqo", 128, "mv", 256, False, True)
+        else:
+            quant("sqn", 0, 128, s, 0)
+            mm(2, 128, "sqn", 0, "mv", 128)
+        cp(B("ix" + p), ps(2, 0, ST[p]))
+        tt(B("lf" + p), ("@", B("t1"), B("ix" + p)), B("ac" + p), A.add)
+        cp(B("li" + p), B("lf" + p))
+
+    def pieces(p):
+        nc, st, n = NP[p] // 32, ST[p], NP[p]
+        w = 16 * nc
+        for e in range(16):
+            b = B("id" + p) if e == 0 else B("xw" + p, w * e - w, w * e)
+            cp(B("xw" + p, w * e, w * e + w), ("@", b, B("li" + p, st * e, st * e + nc)), CHAIN[p])
+        latch(B("tw" + p), B("xw" + p, 15 * w, 16 * w))
+        tt(B("tv" + p), B("tw" + p, 15, w, 16), B("cb" + p), A.subtract)
+        cp(B("tl" + p, 0, 2 * nc, 2), B("tv" + p))
+        for s in range(2 * nc):
+            b, j = 16 * s + (8 if s > nc else 0), 2 * (s % nc)
+            cp(B("ta" + p, 16 * s + 16, 16 * s + 32), ("@", B("ta" + p, b, b + 8), B("tl" + p, j, j + 1)), CHAIN[p])
+        cp(B("lr" + p), ("@", B("xw" + p), B("f1" + p)), "x")
+        latch(B("lw" + p), B("lr" + p))
+        ts(B("ll" + p), B("lw" + p, 15, n, 16), CORR, A.subtract)
+
+    def rows_own():
+        pieces("o")
+        cp(B("rr"), ("@", B("tao"), B("llo")), "x")
+        latch(B("rv"), B("rr"))
+        ts(B("rlst"), B("rv", 15, 224, 16), CORR, A.subtract)
+
+    def rows_new():
+        pieces("n")
+        cp(B("row", 0, 96), ("@", B("tan"), B("lln")), "x")
+        cp(B("row", 96, 320), ("@", B("tan", 104, 112), B("rlst")), "x")
+        latch(B("rol"), B("row"))
+        tt(B("rxf"), B("rol", 15, 320, 16), B("cn"), A.subtract)
+        cp(B("rx"), B("rxf"))
+        ts(B("r64"), B("rol", 15, 320, 16), CORR, A.subtract, 64.0, A.mult)
+        ts(B("r64"), B("r64"), CORR, A.subtract)
+
+    def scores(p):
+        n = NP[p]
+        tt(B("sx" + p), ps(0, 0, n), B("mk", 0, n), A.mult)
+        scan(B("so" + p), B("dr", 0, n), B("sx" + p), A.mult, A.add)
+        ab, z = B("ab" + p), "zz" + p
+        op("s", [ps(1, 0, n)], [ab], lambda e: e.activation(view(ab), view(ps(1, 0, n)), ACT.Abs, bias=2.0 ** -120, scale=0.6 * 2.0 ** -23), acost(ab, []))
+        cp(B(z, 0, n), ps(1, 0, n), "s")
+        if p == "n":
+            tt(B(z, 96, 192), ps(0, 0, n), ab, A.add)
+        tt(B("am" + p), ab, B("ml" if p == "n" else "mg", 0, n), A.mult)
+        tt(B("sg" + p), ps(0, 0, n), B("am" + p), A.add if p == "n" else A.subtract)
+
+    def parts_out(p, x, xlo):
+        c0, n = (96, 224) if p == "o" else (0, 96)
+        for b in range(4):
+            mm(4 + b, max(n, 128), "eq", 128 * b, x, xlo)
+        for b in range(4):
+            cp(B("win", 4 * c0 + b, 4 * (c0 + n), 4), ps(4 + b, 0, n), "x")
+
+    def turn(p, r):
+        lo, hi = (384, 1280) if p == "o" else (0, 384)
+        for s in range(1, 8):
+            o = 1280 * s
+            for d0, d1, s0 in ((0, 128 - 16 * s, 16 * s), (128 - 16 * s, 128, 0)):
+                dma("y", "f%s%d" % (p, r), [("win", lo, hi, 1)], [("win", o + lo, o + hi, 1)], T.win[d0:d1, o + lo:o + hi], T.win[s0:s0 + d1 - d0, lo:hi], 14000.0 if p == "o" else 9000.0)
+
+    turns = []
+
+    def count(i, acc):
+        n = 320 * (len(turns) % 4)
+        turns.append(0)
+        j = B("jk", n, n + width(i))
+        op("s", [i], [j, acc], lambda e: e.activation(view(j), view(i), ACT.Copy, accum_out=view(acc)), 20 + acost(j, []))
+
+    def compare_own():
+        for k in range(14):
+            own = B("soo", 16 * k + 15, 16 * k + 16)
+            o = 896 * (k // 4) + k % 4
+            for z, lo, hi, f in (("sgo", 16 * k, 16 * k + 16, A.is_lt), ("zzo", 16 * k + 16, 224, A.is_le)):
+                if lo < hi:
+                    ts(B("go", o + 4 * lo, o - k % 4 + 4 * hi, 4), B(z, lo, hi), own, f)
+            if k < 13:
+                count(B("go", o + 4 * (16 * k + 16), o - k % 4 + 896, 4), B("aft", k, k + 1))
+        for q in range(4):
+            lo = min(64 * q, 96)
+            quant("gq", 224 * q + lo, 224 * q + 224, "go", 896 * q + 4 * lo)
+            mm(3, 224, "cc", 0, "gq", 224 * q, q == 0, False)
+
+    def compare_new():
+        for k in range(6):
+            own = B("son", 16 * k + 15, 16 * k + 16)
+            q, t = divmod(k, 4)
+            o = 1280 * q
+            ts(B("gn", o + t, o + 896, 4), B("zzo"), own, A.is_gt)
+            ts(B("gn", o + 896 + t, o + 1216, 4), B("zzn", 16 * k + 16, 96 + 16 * k), own, A.is_gt)
+            ts(B("gn", o + 1216 + t, o + 1280, 4), B("sgn", 16 * k, 16 * k + 16), own, A.is_gt)
+            count(B("gn", o + t, o + 1280, 4), B("acl", k, k + 1))
+        for q in range(2):
+            quant("gw", 224 * q, 224 * q + 224, "gn", 1280 * q)
+            mm(3, 224, "cc", 128, "gw", 224 * q, False, q == 1)
+
+    def early(r):
+        x = "qt%d" % r
+        products("o", x, 96)
+        calls("o")
+        scores("o")
+        parts_out("o", x, 96)
+        turn("o", r)
+        compare_own()
+        rows_own()
+
+    def late(r, x):
+        products("n", x, 0)
+        calls("n")
+        scores("n")
+        parts_out("n", x, 0)
+        turn("n", r)
+        compare_new()
+        cp(B("rk16", 0, 6), B("acl"))
+        tt(B("rkc"), B("aft"), B("cs"), A.add)
+        latch(B("cl"), ps(3, 0, 224))
+        tt(B("rko"), B("cl", 15, 224, 16), B("rkc"), A.subtract)
+        cp(B("rk16", 6, 20), B("rko"))
+        op("v", [B("rk16"), B("sd")], [B("ob")], lambda e: e.tensor_copy(view(B("ob")).indirect(view(B("rk16"))), view(B("sd"))), 50 + 3.3 * CY * 320)
+        latch(B("ol"), B("ob"))
+        cp(B("ow", 0, 20), B("ol", 15, 320, 16))
+        for s in range(1, 8):
+            for d0, d1, s0 in ((0, 128 - 16 * s, 16 * s), (128 - 16 * s, 128, 0)):
+                dma("y" if s % 2 else "s", "od%d" % r, [B("ow", 0, 20)], [B("ow", 20 * s, 20 * s + 20)], T.ow[d0:d1, 20 * s:20 * s + 20], T.ow[s0:s0 + d1 - d0, 0:20])
+        rows_new()
+        cp(B("os1"), ("@", B("ow"), B("rx")), "x")
+        latch(B("os2"), B("os1"))
+        tt(B("fo"), B("os2", 15, 320, 16), B("r64"), A.add)
+        for b in range(4):
+            ts(B("fl%d" % b), B("fo"), float(b), A.add)
+        t = "qt%d" % (r + 1)
+        for (l0, l1) in ((0, 8), (8, 20)):
+            for b in range(4):
+                cp(B("tb", 64 * l0 + b, 64 * l1, 4), ("@", B("win"), B("fl%d" % b, l0, l1)), "x")
+            quant(t, 16 * l0, 16 * l1, "tb", 64 * l0)
+            if l0 == 0:
+                send(r + 1)
+
+    def send(r):
+        t = "qt%d" % r
+        dst = T.cores[(rank + r) % len(T.cores)]
+        rid, pid = topo.addr(dst)[:2]
+        m = topo.mask(core, dst)
+
+        def fn():
+            K["need"]("g", [B(t + "c", 0, 96), B(t + "s", 0, 96)], [], "ls", True)
+            for k in "cs":
+                o, i = T["ld%d%s" % (r, k)][:, 0:96], T[t + k][:, 0:96]
+                if k == "c":
+                    o, i = o.bitcast(dt.uint8), i.bitcast(dt.uint8)
+                g.remote_dma(o, i, T.sem["rc%d" % r], T.sem["ls"], pid, rid, m)
+                K["total"]["ls"] = K["total"].get("ls", 0) + len(topo.engines(core, dst))
+        raw("g", [B(t + "c", 0, 96), B(t + "s", 0, 96)], [("sent%d" % r, 0, 1, 1)], fn, 600.0, 2000.0)
+
+    def arrive(r):
+        frm = T.cores[(rank - r) % len(T.cores)]
+        n = 2 * len(topo.engines(frm, core))
+        raw("t", [("sent%d" % r, 0, 1, 1)], [B("ld%dc" % r, 0, 96), B("ld%ds" % r, 0, 96)], lambda: K["wait"]("t", "rc%d" % r, n, {}), 1.0, 0.0)
+        for b in range(4):
+            a = (0, 1, 2, 0)[b]
+            mm(4 + b, 128, "wq", 128 * b, "ld%d" % r, 0)
+            mm(a, 128, "eq", 128 * b, "ld%d" % r, 0)
+            o, i = B("rl", 96 * b, 96 * b + 96), ps(4 + b, 0, 96)
+            op("s", [i], [o], lambda e, o=o, i=i: e.activation(view(o), view(i), ACT.Relu, scale=0.03125), acost(o, []))
+            tt(B("xnb", b, 384, 4), o, ps(a, 0, 96), A.add)
+        quant("xn%d" % r, 0, 128, "xnb", 0)
+
+    early(0)
+    late(0, "qt0")
+    for r in (1, 2):
+        early(r)
+        arrive(r)
+        late(r, "xn%d" % r)
+    x = "qt3"
+    mm(3, 224, "vq", 0, x, 96)
+    cp(B("yb", 96, 320), ps(3, 0, 224), "s")
+    ts(B("rwa"), B("row"), 0.05, A.mult, G_, A.add)
+    cp(B("rwi"), B("rwa"))
+    ts(B("rwa"), B("rwi"), 7.5, A.is_ge, -8.0, A.mult)
+    tt(B("rwb"), B("rwa"), B("rwi"), A.add)
+    dma("y", "out", [B(x + "c", 96, 320)], [], T.oc[:, 384:1280], T[x + "c"][:, 96:320].bitcast(dt.uint8))
+    for k in range(4):
+        dma("y", "out", [B(x + "s", 96, 320)], [], T.osc[4 * k:4 * k + 4, 96:320], T[x + "s"][32 * k:32 * k + 4, 96:320])
+    dma("y", "out", [B("yb", 96, 320)], [], T.y[:, 96:320], T.yb[:, 96:320])
+    dma("s", "out", [B("rwb")], [], T.rw[:, :], T.rwb[0:128:16, :])
+    arrive(3)
+    x = "xn3"
+    mm(3, 128, "vq", 0, x, 0)
+    cp(B("yb", 0, 96), ps(3, 0, 96), "s")
+    dma("s", "out", [B(x + "c", 0, 96)], [], T.oc[:, 0:384], T[x + "c"][:, 0:96].bitcast(dt.uint8))
+    for k in range(4):
+        dma("s" if k % 2 else "y", "out", [B(x + "s", 0, 96)], [], T.osc[4 * k:4 * k + 4, 0:96], T[x + "s"][32 * k:32 * k + 4, 0:96])
+    dma("y", "out", [B("yb", 0, 96)], [], T.y[:, 0:96], T.yb[:, 0:96])
+    K["run"]()
+    for sem, n in sorted(K["total"].items()):
+        K["wait"]("g", sem, n, {})

@@ -1,4 +1,4 @@
-from concourse.mybir import dt, AluOpType, ActivationFunctionType
+from concourse.mybir import dt, AluOpType, AxisListType, ActivationFunctionType
 
 STEP = 16384.0
 LOW = 4194304.0
@@ -36,13 +36,13 @@ def _scratch():
             mx("xn%d" % r, 128)
     for n in ("pi", "gi", "ii", "e1", "e2", "e3", "e4", "i7i"):
         sb(n, 1, I32)
-    for n in ("m16", "mk", "ml", "mg", "dr", "dl", "sd", "ob", "ol", "row", "rol", "os1", "os2", "yb", "rwa", "rwb"):
+    for n in ("m16", "dr", "dl", "sd", "ob", "ol", "row", "rol", "ro4", "os1", "os2", "yb", "rwa", "rwb"):
         sb(n, 320)
     for n in ("chf", "m8", "k8", "d8", "cht", "chs", "t1"):
         sb(n, 64)
-    for n, w in (("cf", 48), ("rl", 384), ("bt0", 3), ("bt1", 3), ("cn", 20), ("nn", 128), ("m64", 512), ("ones", 128), ("eye", 128), ("ulf", 8),
-                 ("clo", 8), ("chh", 8), ("rr", 224), ("rv", 224), ("acl", 6), ("aft", 14), ("cs", 14), ("rkc", 14), ("rko", 14), ("cl", 224),
-                 ("ow", 160), ("rxf", 20), ("r64", 20), ("fo", 20)):
+    for n, w in (("mk", 224), ("mg", 224), ("ml", 96), ("cf", 48), ("rl", 384), ("bt0", 3), ("bt1", 3), ("cn", 20), ("nn", 128), ("m64", 512),
+                 ("ones", 128), ("eye", 128), ("ulf", 8), ("clo", 8), ("chh", 8), ("rr", 224), ("rv", 224), ("acl", 6), ("aft", 14), ("cs", 14),
+                 ("rkc", 14), ("rko", 14), ("cl", 224), ("ow", 160), ("rxf", 20)):
         sb(n, w)
     sb("chi", 64, I32), sb("chb", 64, I32), sb("rwi", 320, I32)
     for n, w in (("ul", 8), ("rlst", 14), ("rk16", 20), ("rx", 20), ("fl0", 20), ("fl1", 20), ("fl2", 20), ("fl3", 20)):
@@ -186,7 +186,7 @@ def _make(g, T):
                 after[k].append(i)
         way = [0.0] * n
         for i in range(n - 1, -1, -1):
-            way[i] = jobs[i]["cost"] + jobs[i]["lat"] + max([way[k] + 50.0 for k in after[i]] or [0.0])
+            way[i] = jobs[i]["cost"] + jobs[i]["lat"] + max([way[k] + 100.0 for k in after[i]] or [0.0])
         free = {q: 0.0 for q in queues}
         fin, qof, left = {}, {}, [len(j["pre"]) for j in jobs]
         ready = [i for i in range(n) if not left[i]]
@@ -196,7 +196,7 @@ def _make(g, T):
                 for q in (("v", "s") if jobs[i]["q"] == "x" else (jobs[i]["q"],)):
                     t = 0.0
                     for k in jobs[i]["pre"]:
-                        t = max(t, fin[k] + (25.0 if qof[k] == q else 70.0))
+                        t = max(t, fin[k] + (80.0 if qof[k] == q else 150.0))
                     key = (max(free[q], t - SLACK), -way[i], max(free[q], t))
                     if best is None or key < best[0]:
                         best = (key, i, q)
@@ -363,11 +363,13 @@ def rank_program(g, core, T, topo):
         cp(cf(j), B(n))
     ts(CORR, I_, -STEP, A.mult, 15.0 * STEP, A.add)
     ts(NCORR, CORR, -1.0, A.mult)
+    for b in range(4):
+        ts(cf(40 + b), NCORR, float(b), A.add)
     ts(H8, I_, 8.0, A.is_ge)
     ts(H88, H8, 8.0, A.mult)
-    ts(B("mk"), B("m16"), I_, A.is_equal)
-    ts(B("ml"), B("m16"), I_, A.is_lt)
-    ts(B("mg"), B("m16"), I_, A.is_gt)
+    ts(B("mk"), B("m16", 0, 224), I_, A.is_equal)
+    ts(B("ml"), B("m16", 0, 96), I_, A.is_lt)
+    ts(B("mg"), B("m16", 0, 224), I_, A.is_gt)
     ts(B("dr"), B("m16"), 0.0, A.is_gt)
     t0, t1, t2, t3, t4, t5, RN, RA, RB, FN, FA = (cf(j) for j in range(11, 22))
     ts(t0, G_, 3.0, A.is_ge)
@@ -387,14 +389,14 @@ def rank_program(g, core, T, topo):
     for n, r in (("mao", RA), ("mb", RB), ("man", RN)):
         ts(B(n), B("m16", 0, 128), r, A.is_equal)
     fill(B("mvb"), 0.0)
-    fill(B("sto"), 0.0)
-    fill(B("stn"), 0.0)
+    fill(B("sto", 3, 1024, 4), 0.0)
+    fill(B("stn", 3, 512, 4), 0.0)
     for t, w in enumerate((4.0, 2.0, 1.0)):
         ts(cf(22 + t), FN, w, A.mult)
         ts(cf(25 + t), FA, w, A.mult)
-        ts(B("mvb", t, 512, 4), B("nn"), E3, A.is_equal, cf(25 + t), A.mult)
-        ts(B("mvb", 512 + t, 1024, 4), B("nn"), E4, A.is_equal, cf(22 + t), A.mult)
-        ts(B("mvb", 1024 + t, 1536, 4), B("nn"), E3, A.is_equal, w, A.mult)
+        ts(B("mvb", t, 32, 4), B("nn", 0, 8), E3, A.is_equal, cf(25 + t), A.mult)
+        ts(B("mvb", 512 + t, 544, 4), B("nn", 0, 8), E4, A.is_equal, cf(22 + t), A.mult)
+        ts(B("mvb", 1024 + t, 1056, 4), B("nn", 0, 8), E3, A.is_equal, w, A.mult)
     quant("mv", 0, 384, "mvb", 0)
     ts(B("dl"), B("m16"), I_, A.is_gt, LOW + STEP, A.mult)
     ts(B("dl"), B("dl"), -LOW, A.add)
@@ -407,7 +409,8 @@ def rank_program(g, core, T, topo):
         fill(B("go", 896 * q + 4 * min(64 * q, 96), 896 * q + 4 * min(64 * q + 64, 224)), 0.0)
         if q:
             quant("gq", 224 * q, 224 * q + 128, "zb", 0)
-    fill(B("gn", 1280, 2560), 0.0)
+    for t in (2, 3):
+        fill(B("gn", 1280 + t, 2560, 4), 0.0)
     fill(B("aft"), 0.0)
     iota(B("cs"), [[16, 14]], -304)
     ts(B("cs"), B("cs"), CORR, A.add)
@@ -448,7 +451,7 @@ def rank_program(g, core, T, topo):
     ts(B("sd"), B("sd"), NCORR, A.add)
     iota(B("cn"), [[-1, 20]])
     ts(B("cn"), B("cn"), CORR, A.add)
-    fill(B("xnb"), 0.0)
+    fill(B("xnb", 384, 512), 0.0)
     quant("zq", 0, 128, "zb", 0)
     for r in range(1, ROUNDS + 1):
         dma("y", "zf", [B("zqc", 0, 32)], [B("ld%dc" % r, 96, 128)], T["ld%dc" % r][:, 96:128].bitcast(dt.uint8), T.zqc[:, 0:32].bitcast(dt.uint8))
@@ -510,8 +513,7 @@ def rank_program(g, core, T, topo):
         latch(B("rol"), B("row"))
         tt(B("rxf"), B("rol", 15, 320, 16), B("cn"), A.subtract)
         cp(B("rx"), B("rxf"))
-        ts(B("r64"), B("rol", 15, 320, 16), CORR, A.subtract, 64.0, A.mult)
-        ts(B("r64"), B("r64"), CORR, A.subtract)
+        ts(B("ro4"), B("row"), 64.0, A.mult)
 
     def scores(p):
         n = NP[p]
@@ -545,7 +547,12 @@ def rank_program(g, core, T, topo):
         n = 320 * (len(turns) % 4)
         turns.append(0)
         j = B("jk", n, n + width(i))
-        op("s", [i], [j, acc], lambda e: e.activation(view(j), view(i), ACT.Copy, accum_out=view(acc)), 20 + acost(j, []))
+
+        def fn(e):
+            if e is g.vector:
+                return e.tensor_reduce(view(acc), view(i), AxisListType.X, A.add)
+            return e.activation(view(j), view(i), ACT.Copy, accum_out=view(acc))
+        op("x", [i], [j, acc], fn, 20 + acost(j, []))
 
     def compare_own():
         for k in range(14):
@@ -601,13 +608,12 @@ def rank_program(g, core, T, topo):
         cp(B("ow", 0, 20), B("ol", 15, 320, 16))
         for s in range(1, 8):
             for d0, d1, s0 in ((0, 128 - 16 * s, 16 * s), (128 - 16 * s, 128, 0)):
-                dma("y" if s % 2 else "s", "od%d" % r, [B("ow", 0, 20)], [B("ow", 20 * s, 20 * s + 20)], T.ow[d0:d1, 20 * s:20 * s + 20], T.ow[s0:s0 + d1 - d0, 0:20])
+                dma("y" if s % 2 else "s", "od%d" % r, [B("ow", 0, 20)], [B("ow", 20 * s, 20 * s + 20)], T.ow[d0:d1, 20 * s:20 * s + 20], T.ow[s0:s0 + d1 - d0, 0:20], 3500.0)
         rows_new()
-        cp(B("os1"), ("@", B("ow"), B("rx")), "x")
+        tt(B("os1"), ("@", B("ow"), B("rx")), B("ro4"), A.add)
         latch(B("os2"), B("os1"))
-        tt(B("fo"), B("os2", 15, 320, 16), B("r64"), A.add)
         for b in range(4):
-            ts(B("fl%d" % b), B("fo"), float(b), A.add)
+            ts(B("fl%d" % b), B("os2", 15, 320, 16), cf(40 + b), A.add)
         t = "qt%d" % (r + 1)
         for (l0, l1) in ((0, 8), (8, 20)):
             for b in range(4):

from concourse.mybir import dt, AluOpType, AxisListType, ActivationFunctionType

STEP = 16384.0
LOW = 4194304.0
SLACK = 60.0
CY = 0.83
CHAIN = {"o": "s", "n": "x"}
ROUNDS = 3
NP = {"o": 224, "n": 96}
ST = {"o": 8, "n": 4}
F32, BF, I32, U16 = "float32", "bfloat16", "int32", "uint16"
CODE, SC = "float8_e4m3fn_x4", "uint8"


def _scratch():
    d = {}

    def sb(name, n, t=F32):
        d[name] = ("sbuf", [128, n], t)

    def mx(name, n):
        sb(name + "c", n, CODE)
        sb(name + "s", n, SC)
    for b in range(8):
        d["ps%d" % b] = ("psum", [128, 512], F32)
    for n, w in (("xb", 1280), ("ub", 512), ("vb", 512), ("eb", 2048), ("mvb", 1536), ("zb", 512), ("ccb", 1024), ("xnb", 512), ("tb", 1280),
                 ("win", 10240), ("sto", 1024), ("stn", 512), ("mao", 128), ("man", 128), ("mb", 128), ("go", 3584), ("gn", 2560), ("jk", 1280)):
        sb(n, w, BF)
    for n, w in (("uq", 128), ("ur", 128), ("vq", 128), ("eq", 512), ("mv", 384), ("zq", 128), ("wq", 512), ("cc", 256), ("sqo", 256), ("sqn", 128),
                 ("gq", 896), ("gw", 448)):
        mx(n, w)
    for r in range(ROUNDS + 1):
        mx("qt%d" % r, 320)
        if r:
            mx("ld%d" % r, 128)
            mx("xn%d" % r, 128)
    for n in ("pi", "gi", "ii", "e1", "e2", "e3", "e4", "i7i"):
        sb(n, 1, I32)
    for n in ("m16", "dr", "dl", "sd", "ob", "ol", "row", "rol", "ro4", "os1", "os2", "yb", "rwa", "rwb"):
        sb(n, 320)
    for n in ("chf", "m8", "k8", "d8", "cht", "chs", "t1"):
        sb(n, 64)
    for n, w in (("mk", 224), ("mg", 224), ("ml", 96), ("cf", 48), ("rl", 384), ("bt0", 3), ("bt1", 3), ("cn", 20), ("nn", 128), ("m64", 512),
                 ("ones", 128), ("eye", 128), ("ulf", 8), ("clo", 8), ("chh", 8), ("rr", 224), ("rv", 224), ("acl", 6), ("aft", 14), ("cs", 14),
                 ("rkc", 14), ("rko", 14), ("cl", 224), ("ow", 160), ("rxf", 20)):
        sb(n, w)
    sb("chi", 64, I32), sb("chb", 64, I32), sb("rwi", 320, I32)
    for n, w in (("ul", 8), ("rlst", 14), ("rk16", 20), ("rx", 20), ("fl0", 20), ("fl1", 20), ("fl2", 20), ("fl3", 20)):
        sb(n, w, U16)
    for p, n in NP.items():
        S, nc, st = n // 16, n // 32, ST[p]
        for k, w in (("id", 16 * nc), ("xw", 256 * nc), ("tw", 16 * nc), ("tv", nc), ("lf", 16 * st), ("ac", 16 * st), ("ta", 16 * S + 16), ("cb", nc),
                     ("f1f", S), ("lr", n), ("lw", n), ("zz", 224 if p == "o" else 192), ("ab", n), ("am", n), ("sx", n), ("so", n), ("sg", n)):
            sb(k + p, w)
        for k, w in (("ix", st), ("li", 16 * st), ("tl", 2 * nc), ("f1", S), ("ll", S)):
            sb(k + p, w, U16)
    return d


def _pack(d):
    place, at, rest = {}, {}, {}
    for name, (where, shape, t) in d.items():
        host = {F32: "kf", U16: "ku", I32: "ki"}.get(t)
        if where != "sbuf" or host is None or name in ("chi", "ow", "yb", "rwb"):
            rest[name] = (where, shape, t)
            continue
        place[name] = (host, at.get(host, 0))
        at[host] = at.get(host, 0) + (shape[1] + 15) // 16 * 16
    for host, t in (("kf", F32), ("ku", U16), ("ki", I32)):
        rest[host] = ("sbuf", [128, at[host]], t)
    return rest, place


BUFS = _scratch()
SCRATCH, PLACE = _pack(BUFS)
SEMAPHORES = (["cv", "ct", "cs", "cg", "dx", "du", "dv", "dw", "dc", "zf", "out", "ls"]
              + [k + "%d" % r for k in ("fo", "fn", "od") for r in range(3)] + ["rc%d" % r for r in range(1, 4)])


def _make(g, T):
    queues = {"v": g.vector, "t": g.tensor, "s": g.scalar, "g": g, "y": g.sync}
    comp = {"v": "cv", "t": "ct", "s": "cs", "g": "cg"}
    total, known, recs, jobs = {}, {q: {} for q in queues}, {}, []

    def view(a):
        n, lo, hi, st = a
        return T[n][:, lo:hi] if st == 1 else T[n][:, lo:hi:st]

    def span(a):
        return (a[0], 0, 512, 1, True) if a[0][:2] == "ps" else (a[0], a[1], a[2], a[3], False)

    def meet(lo, hi, st, x):
        return x[0] < hi and lo < x[1] and not (st == x[2] and st > 1 and (lo - x[0]) % st)

    def cover(lo, hi, st, x):
        return lo <= x[0] and x[1] <= hi and (st == 1 or (st == x[2] and (lo - x[0]) % st == 0))

    def wait(q, sem, val, clk):
        k = known[q]
        if k.get(sem, 0) >= val:
            return
        queues[q].wait_ge(T.sem[sem], int(val))
        k[sem] = val
        for s, x in clk.items():
            if k.get(s, 0) < x:
                k[s] = x

    def need(q, reads, writes, sem, self_ok):
        deps = []
        for lst, isw in ((reads, False), (writes, True)):
            for a in lst:
                n, lo, hi, st, ps = span(a)
                for x in recs.get(n, []):
                    rw, rq, rsem = x[3], x[4], x[5]
                    if not meet(lo, hi, st, x) or not (isw or rw or (ps and rq != q)):
                        continue
                    if rq == q == "t" and rw and isw:
                        continue
                    if rsem == sem and not self_ok:
                        continue
                    deps.append((rsem, x[6], x[7]))
        deps.sort(key=lambda d: -sum(d[2].values()))
        for s, v, c in deps:
            wait(q, s, v if s in comp.values() else total[s], c)

    def note(q, reads, writes, sem, val):
        clk = dict(known[q])
        for lst, isw in ((reads, False), (writes, True)):
            for a in lst:
                n, lo, hi, st, ps = span(a)
                old = recs.get(n, [])
                if isw:
                    old = [x for x in old if not cover(lo, hi, st, x) or (x[5] == sem and sem not in comp.values())]
                else:
                    old = [x for x in old if not (not x[3] and x[4] == q and x[5] == sem and cover(lo, hi, st, x))]
                recs[n] = old + [(lo, hi, st, isw, q, sem, val, clk)]

    def put(q, reads, writes, fn):
        sem = comp[q]
        need(q, reads, writes, sem, True)
        total[sem] = total.get(sem, 0) + 1
        fn(queues[q]).then_inc(T.sem[sem], 1)
        note(q, reads, writes, sem, total[sem])

    def put_dma(q, sem, reads, writes, out, in_):
        need(q, reads, writes, sem, False)
        total[sem] = total.get(sem, 0) + 16
        queues[q].dma_start(out, in_).then_inc(T.sem[sem], 16)
        note(q, reads, writes, sem, total[sem])

    def op(q, reads, writes, fn, cost=60.0):
        jobs.append(dict(q=q, r=reads, w=writes, fn=fn, cost=cost, lat=0.0, sem=None))

    def dma(q, sem, reads, writes, out, in_, lat=2000.0):
        jobs.append(dict(q=q, r=reads, w=writes, fn=(out, in_), cost=60.0, lat=lat, sem=sem))

    def raw(q, reads, writes, fn, cost, lat):
        jobs.append(dict(q=q, r=reads, w=writes, fn=fn, cost=cost, lat=lat, sem="raw"))

    def run():
        table, groups, n = {}, {}, len(jobs)
        for i, j in enumerate(jobs):
            pre = set()
            grp = j["sem"] if j["sem"] not in (None, "raw") else None
            acc = [(span(a), False) for a in j["r"]] + [(span(a), True) for a in j["w"]]
            for (nm, lo, hi, st, ps), isw in acc:
                for x in table.get(nm, []):
                    k = x[4]
                    if k != i and meet(lo, hi, st, x) and (x[3] or isw or ps) and (grp is None or jobs[k]["sem"] != grp):
                        pre.add(k)
            for (nm, lo, hi, st, ps), isw in acc:
                old = table.get(nm, [])
                if isw and grp is None:
                    old = [x for x in old if not cover(lo, hi, st, x)]
                table[nm] = old + [(lo, hi, st, isw, i)]
            for k in list(pre):
                if jobs[k]["sem"] not in (None, "raw"):
                    pre.update(groups[jobs[k]["sem"]])
            pre.discard(i)
            j["pre"] = pre
            if grp:
                groups.setdefault(grp, []).append(i)
        after = [[] for _ in jobs]
        for i, j in enumerate(jobs):
            for k in j["pre"]:
                after[k].append(i)
        way = [0.0] * n
        for i in range(n - 1, -1, -1):
            way[i] = jobs[i]["cost"] + jobs[i]["lat"] + max([way[k] + 100.0 for k in after[i]] or [0.0])
        free = {q: 0.0 for q in queues}
        fin, qof, left = {}, {}, [len(j["pre"]) for j in jobs]
        ready = [i for i in range(n) if not left[i]]
        while ready:
            best = None
            for i in ready:
                for q in (("v", "s") if jobs[i]["q"] == "x" else (jobs[i]["q"],)):
                    t = 0.0
                    for k in jobs[i]["pre"]:
                        t = max(t, fin[k] + (80.0 if qof[k] == q else 150.0))
                    key = (max(free[q], t - SLACK), -way[i], max(free[q], t))
                    if best is None or key < best[0]:
                        best = (key, i, q)
            key, i, q = best
            j = jobs[i]
            ready.remove(i)
            free[q] = key[2] + j["cost"]
            fin[i] = free[q] + j["lat"]
            qof[i] = q
            if j["sem"] is None:
                put(q, j["r"], j["w"], j["fn"])
            elif j["sem"] == "raw":
                j["fn"]()
            else:
                put_dma(q, j["sem"], j["r"], j["w"], j["fn"][0], j["fn"][1])
            for k in after[i]:
                left[k] -= 1
                if not left[k]:
                    ready.append(k)
        jobs.clear()
    return dict(view=view, wait=wait, need=need, op=op, dma=dma, raw=raw, run=run, total=total)


def rank_program(g, core, T, topo):
    rank = T.rank_of(core)
    if rank is None:
        return
    K = _make(g, T)
    view, op, dma, raw = K["view"], K["op"], K["dma"], K["raw"]
    A, ACT = AluOpType, ActivationFunctionType

    def B(n, lo=0, hi=None, st=1):
        h, at = PLACE.get(n, (n, 0))
        return (h, at + lo, at + (BUFS[n][1][1] if hi is None else hi), st)

    def cf(j):
        return B("cf", j, j + 1)

    def ps(b, lo, hi):
        return ("ps%d" % b, lo, hi, 1)

    def width(a):
        return (a[2] - a[1] + a[3] - 1) // a[3]

    def small(a):
        return SCRATCH[a[0]][2] in (BF, U16)

    def vc(out, ins, two=False):
        n = width(out)
        if any(a[0] == "@" for a in ins):
            return 50 + 1.5 * CY * n
        if two and not any(a[0][:2] == "ps" for a in ins):
            return max(64, 2 * n) * CY
        return max(64, n * (0.5 if small(out) and all(small(a) for a in ins) else 1.0)) * CY

    def acost(out, ins):
        return (65 + 1.5 * CY * width(out)) if any(a[0] == "@" for a in ins) else 50 + CY * width(out)

    def sc(x):
        return (view(x), [x]) if isinstance(x, tuple) else (x, [])

    def src(a):
        if a[0] == "@":
            return view(a[1]).indirect(view(a[2])), [a[1], a[2]]
        return view(a), [a]

    def ts(out, in0, s1, op0, s2=None, op1=None):
        iv, ir = src(in0)
        (x1, r1), (x2, r2) = sc(s1), sc(s2)

        def vec(e):
            if op1 is None:
                return e.tensor_scalar(view(out), iv, x1, None, op0)
            return e.tensor_scalar(view(out), iv, x1, x2, op0, op1)

        def either(e):
            if e is g.vector:
                return vec(e)
            m, a = (x1, 0.0 if op1 is None else x2) if op0 == A.mult else (1.0, x1)
            return e.activation(view(out), iv, ACT.Identity, bias=a, scale=m)
        plain = SCRATCH[out[0]][2] == F32 and SCRATCH[in0[0]][2] == F32 and (op0 == A.mult and op1 in (None, A.add) or op0 == A.add and op1 is None)
        if plain:
            op("x", ir + r1 + r2, [out], either, 10 + vc(out, [in0]))
        else:
            op("v", ir + r1 + r2, [out], vec, vc(out, [in0]))

    def tt(out, in0, in1, o):
        iv, ir = src(in0)
        op("v", ir + [in1], [out], lambda e: e.tensor_tensor(view(out), iv, view(in1), o), vc(out, [in0, in1], True))

    def cp(out, in_, q="v"):
        iv, ir = src(in_)

        def fn(e):
            if e is g.vector:
                return e.tensor_copy(view(out), iv)
            return e.activation(view(out), iv, ACT.Copy)
        op(q, ir, [out], fn, vc(out, [in_]) if q == "v" else acost(out, [in_]))

    def lay(out, in_, col):
        def fn(e):
            if e is g.vector:
                return e.tensor_scalar(view(out), view(in_), view(col), None, A.mult)
            return e.activation(view(out), view(in_), ACT.Copy, scale=view(col))
        op("x", [in_, col], [out], fn, 90.0)

    def scan(out, d0, d1, o0, o1):
        op("v", [d0, d1], [out], lambda e: e.tensor_tensor_scan(view(out), view(d0), view(d1), 0.0, o0, o1), CY * width(out))

    def latch(out, d1):
        scan(out, B("dl", 0, width(d1)), d1, A.add, A.max)

    def fill(out, x):
        op("v", [], [out], lambda e: e.memset(view(out), x), vc(out, []))

    def iota(out, pat, base=0, cm=0):
        if SCRATCH[out[0]][2] == I32:
            op("g", [], [out], lambda e: e.iota(view(out), pat, base, cm), 150.0)
        else:
            op("g", [], [out], lambda e: e.iota(view(out), pat, base, cm, allow_small_or_imprecise_dtypes=True), 130 + 2 * CY * width(out))

    def quant(name, lo, hi, tile, tlo):
        t = (tile, tlo, tlo + 4 * (hi - lo), 1)
        c, s = (name + "c", lo, hi, 1), (name + "s", lo, hi, 1)
        op("v", [t], [c, s], lambda e: e.quantize_mx(view(c), view(s), view(t)), 12 + 0.88 * (hi - lo))

    def mm(bank, n, w, wlo, x, xlo, start=True, stop=True):
        lc, ls = (w + "c", wlo, wlo + 128, 1), (w + "s", wlo, wlo + 128, 1)
        rc, rs = (x + "c", xlo, xlo + n, 1), (x + "s", xlo, xlo + n, 1)
        o = ps(bank, 0, n)
        op("t", [lc, ls, rc, rs], [o], lambda e: e.matmul_mx(view(o), view(lc), view(ls), view(rc), view(rs), start, stop), 0.6 * (n + 16))

    dma("y", "dx", [], [B("xb")], view(B("xb")), T.x[:, :])
    dma("s", "du", [], [B("ub")], view(B("ub")), T.u[:, :])
    dma("y", "dc", [], [B("chi")], T.chi[0:1, 0:64], T.ch[:, :])
    dma("y", "dv", [], [B("vb")], view(B("vb")), T.v[:, :])
    dma("y", "dw", [], [B("wqc")], T.wqc[:, 0:512].bitcast(dt.uint8), T.wc[:, :])
    dma("y", "dw", [], [B("wqs")], view(B("wqs")), T.ws[:, :])

    iota(B("pi"), [[1, 1]], 0, 1)
    iota(B("ulf"), [[16, 8]])
    iota(B("m16"), [[0, 20], [1, 16]])
    iota(B("nn"), [[1, 128]])
    fill(B("eb"), 0.0)
    fill(B("ones"), 1.0)
    op("g", [B("ones")], [B("eye")], lambda e: e.affine_select(view(B("eye")), view(B("ones")), [[-1, 128]], A.is_equal, 0.0, 0, 1), 400.0)
    cp(B("ul"), B("ulf"))
    quant("uq", 0, 128, "ub", 0)
    quant("qt0", 0, 320, "xb", 0)
    op("v", [B("uqc"), B("ul")], [B("urc")], lambda e: e.tensor_copy(T.urc[:, 0:128].bitcast(dt.uint32), T.uqc[:, 0:128].bitcast(dt.uint32).indirect(view(B("ul")))), 210.0)
    op("v", [B("uqs"), B("ul")], [B("urs")], lambda e: e.tensor_copy(T.urs[:, 0:128], T.uqs[:, 0:128].indirect(view(B("ul")))), 210.0)
    for b in range(4):
        cp(B("eb", 512 * b + b, 512 * (b + 1), 4), B("eye"), "x")
    quant("eq", 0, 512, "eb", 0)
    ts(B("gi"), B("pi"), 4, A.arith_shift_right)
    ts(B("ii"), B("pi"), 15, A.bitwise_and)
    ts(B("e1"), B("ii"), 1, A.bitwise_and)
    ts(B("e2"), B("ii"), 3, A.bitwise_and)
    ts(B("e3"), B("ii"), 1, A.arith_shift_right)
    ts(B("e4"), B("ii"), 2, A.arith_shift_right)
    ts(B("i7i"), B("ii"), 7, A.bitwise_and)
    G_, I_, E1, E2, E3, E4, I7, CORR, NCORR, H8, H88 = (cf(j) for j in range(11))
    for j, n in enumerate(("gi", "ii", "e1", "e2", "e3", "e4", "i7i")):
        cp(cf(j), B(n))
    ts(CORR, I_, -STEP, A.mult, 15.0 * STEP, A.add)
    ts(NCORR, CORR, -1.0, A.mult)
    for b in range(4):
        ts(cf(40 + b), NCORR, float(b), A.add)
    ts(H8, I_, 8.0, A.is_ge)
    ts(H88, H8, 8.0, A.mult)
    ts(B("mk"), B("m16", 0, 224), I_, A.is_equal)
    ts(B("ml"), B("m16", 0, 96), I_, A.is_lt)
    ts(B("mg"), B("m16", 0, 224), I_, A.is_gt)
    ts(B("dr"), B("m16"), 0.0, A.is_gt)
    t0, t1, t2, t3, t4, t5, RN, RA, RB, FN, FA = (cf(j) for j in range(11, 22))
    ts(t0, G_, 3.0, A.is_ge)
    ts(FN, t0, -7.0, A.mult, 8.0, A.add)
    ts(t0, t0, -3.0, A.mult, G_, A.add)
    ts(t1, E2, 4.0, A.mult, t0, A.add)
    ts(t2, G_, 6.0, A.is_ge, 100.0, A.mult)
    tt(RN, t1, t2, A.add)
    ts(t3, G_, 7.0, A.is_ge)
    ts(FA, t3, -7.0, A.mult, 8.0, A.add)
    ts(t3, t3, -7.0, A.mult, G_, A.add)
    ts(RA, E1, 8.0, A.mult, t3, A.add)
    ts(t4, E1, 8.0, A.mult, G_, A.add)
    ts(t5, G_, 2.0, A.is_lt, 100.0, A.mult)
    ts(t4, t4, -1.0, A.add)
    tt(RB, t4, t5, A.add)
    for n, r in (("mao", RA), ("mb", RB), ("man", RN)):
        ts(B(n), B("m16", 0, 128), r, A.is_equal)
    fill(B("mvb"), 0.0)
    fill(B("sto", 3, 1024, 4), 0.0)
    fill(B("stn", 3, 512, 4), 0.0)
    for t, w in enumerate((4.0, 2.0, 1.0)):
        ts(cf(22 + t), FN, w, A.mult)
        ts(cf(25 + t), FA, w, A.mult)
        ts(B("mvb", t, 32, 4), B("nn", 0, 8), E3, A.is_equal, cf(25 + t), A.mult)
        ts(B("mvb", 512 + t, 544, 4), B("nn", 0, 8), E4, A.is_equal, cf(22 + t), A.mult)
        ts(B("mvb", 1024 + t, 1056, 4), B("nn", 0, 8), E3, A.is_equal, w, A.mult)
    quant("mv", 0, 384, "mvb", 0)
    ts(B("dl"), B("m16"), I_, A.is_gt, LOW + STEP, A.mult)
    ts(B("dl"), B("dl"), -LOW, A.add)
    iota(B("m64"), [[1, 8], [0, 64]])
    ts(B("ccb", 0, 512), B("m64"), G_, A.is_equal)
    ts(B("ccb", 512, 1024), B("m64"), G_, A.is_equal, -1.0, A.mult)
    quant("cc", 0, 256, "ccb", 0)
    fill(B("zb"), 0.0)
    for q in range(4):
        fill(B("go", 896 * q + 4 * min(64 * q, 96), 896 * q + 4 * min(64 * q + 64, 224)), 0.0)
        if q:
            quant("gq", 224 * q, 224 * q + 128, "zb", 0)
    for t in (2, 3):
        fill(B("gn", 1280 + t, 2560, 4), 0.0)
    fill(B("aft"), 0.0)
    iota(B("cs"), [[16, 14]], -304)
    ts(B("cs"), B("cs"), CORR, A.add)
    op("g", [B("chi")], [B("chb")], lambda e: e.partition_broadcast(view(B("chb")), T.chi[0:1, 0:64], 128), 350.0)
    iota(B("m8"), [[0, 8], [1, 8]])
    cp(B("chf"), B("chb"))
    ts(B("k8"), B("m8"), I7, A.is_equal)
    ts(B("d8"), B("m8"), 0.0, A.is_gt)
    tt(B("cht"), B("chf"), B("k8"), A.mult)
    scan(B("chs"), B("d8"), B("cht"), A.mult, A.add)
    CHV = B("chs", 7, 64, 8)
    ts(B("chh"), CHV, H8, A.mult)
    tt(B("clo"), CHV, B("chh"), A.subtract)
    for a in range(8):
        ts(B("t1", 8 * a, 8 * a + 8), B("chh"), B("clo", a, a + 1), A.add)
    iota(B("tao", 0, 16), [[0, 2], [1, 8]])
    for p in NP:
        nc, j = NP[p] // 32, 28 + 3 * "on".index(p)
        iota(B("id" + p), [[16, nc], [16 * nc + 8, 2], [1, 8]])
        iota(B("id" + p, 8, 16), [[1, 8]], 16 * nc)
        iota(B("ac" + p), [[0, 16], [16, ST[p]]])
        ts(B("ac" + p), B("ac" + p), H88, A.add)
        iota(B("f1f" + p), [[8, 2], [16, nc]])
        ts(cf(j), I_, 16.0 * nc, A.mult, G_, A.add)
        ts(B("f1" + p), B("f1f" + p), cf(j), A.add)
        iota(B("cb" + p), [[16, nc]])
        ts(cf(j + 1), H8, 16.0 * nc + 8, A.mult, CORR, A.add)
        ts(cf(j + 2), H8, 16.0 * nc, A.mult, CORR, A.add)
        ts(B("cb" + p, 1, nc), B("cb" + p, 1, nc), cf(j + 1), A.add)
        ts(B("cb" + p, 0, 1), B("cb" + p, 0, 1), cf(j + 2), A.add)
    TI = B("tan", 0, 16)
    iota(TI, [[0, 2], [1, 8]])
    ts(TI, TI, G_, A.subtract)
    ts(B("rxf", 0, 16), TI, 0.0, A.is_lt, 8.0, A.mult)
    tt(TI, TI, B("rxf", 0, 16), A.add)
    ts(TI, TI, 20.0, A.mult)
    iota(B("sd"), [[4, 320]])
    ts(B("sd"), B("sd"), NCORR, A.add)
    iota(B("cn"), [[-1, 20]])
    ts(B("cn"), B("cn"), CORR, A.add)
    fill(B("xnb", 384, 512), 0.0)
    quant("zq", 0, 128, "zb", 0)
    for r in range(1, ROUNDS + 1):
        dma("y", "zf", [B("zqc", 0, 32)], [B("ld%dc" % r, 96, 128)], T["ld%dc" % r][:, 96:128].bitcast(dt.uint8), T.zqc[:, 0:32].bitcast(dt.uint8))
        dma("y", "zf", [B("zqs", 0, 32)], [B("ld%ds" % r, 96, 128)], T["ld%ds" % r][:, 96:128], T.zqs[:, 0:32])
    quant("vq", 0, 128, "vb", 0)

    def products(p, x, xlo):
        n = 224 if p == "o" else 128
        mm(0, n, "ur", 0, x, xlo)
        mm(1, n, "ur", 0, x, xlo)
        mm(2, 128, x, xlo, "uq", 0)
        if p == "o":
            mm(7, 128, x, xlo + 96, "uq", 0)

    def calls(p):
        s = "st" + p
        for b, m, o in [(2, "ma" + p, 0)] + ([(7, "mb", 512)] if p == "o" else []):
            bits = "bt%d" % (o // 512)
            ts(B(bits), ps(b, 1, 4), 0.0, A.is_gt)
            for t in range(3):
                lay(B(s, o + t, o + 512, 4), B(m), B(bits, t, t + 1))
        if p == "o":
            quant("sqo", 0, 256, s, 0)
            mm(2, 128, "sqo", 0, "mv", 0, True, False)
            mm(2, 128, "sqo", 128, "mv", 256, False, True)
        else:
            quant("sqn", 0, 128, s, 0)
            mm(2, 128, "sqn", 0, "mv", 128)
        cp(B("ix" + p), ps(2, 0, ST[p]))
        tt(B("lf" + p), ("@", B("t1"), B("ix" + p)), B("ac" + p), A.add)
        cp(B("li" + p), B("lf" + p))

    def pieces(p):
        nc, st, n = NP[p] // 32, ST[p], NP[p]
        w = 16 * nc
        for e in range(16):
            b = B("id" + p) if e == 0 else B("xw" + p, w * e - w, w * e)
            cp(B("xw" + p, w * e, w * e + w), ("@", b, B("li" + p, st * e, st * e + nc)), CHAIN[p])
        latch(B("tw" + p), B("xw" + p, 15 * w, 16 * w))
        tt(B("tv" + p), B("tw" + p, 15, w, 16), B("cb" + p), A.subtract)
        cp(B("tl" + p, 0, 2 * nc, 2), B("tv" + p))
        for s in range(2 * nc):
            b, j = 16 * s + (8 if s > nc else 0), 2 * (s % nc)
            cp(B("ta" + p, 16 * s + 16, 16 * s + 32), ("@", B("ta" + p, b, b + 8), B("tl" + p, j, j + 1)), CHAIN[p])
        cp(B("lr" + p), ("@", B("xw" + p), B("f1" + p)), "x")
        latch(B("lw" + p), B("lr" + p))
        ts(B("ll" + p), B("lw" + p, 15, n, 16), CORR, A.subtract)

    def rows_own():
        pieces("o")
        cp(B("rr"), ("@", B("tao"), B("llo")), "x")
        latch(B("rv"), B("rr"))
        ts(B("rlst"), B("rv", 15, 224, 16), CORR, A.subtract)

    def rows_new():
        pieces("n")
        cp(B("row", 0, 96), ("@", B("tan"), B("lln")), "x")
        cp(B("row", 96, 320), ("@", B("tan", 104, 112), B("rlst")), "x")
        latch(B("rol"), B("row"))
        tt(B("rxf"), B("rol", 15, 320, 16), B("cn"), A.subtract)
        cp(B("rx"), B("rxf"))
        ts(B("ro4"), B("row"), 64.0, A.mult)

    def scores(p):
        n = NP[p]
        tt(B("sx" + p), ps(0, 0, n), B("mk", 0, n), A.mult)
        scan(B("so" + p), B("dr", 0, n), B("sx" + p), A.mult, A.add)
        ab, z = B("ab" + p), "zz" + p
        op("s", [ps(1, 0, n)], [ab], lambda e: e.activation(view(ab), view(ps(1, 0, n)), ACT.Abs, bias=2.0 ** -120, scale=0.6 * 2.0 ** -23), acost(ab, []))
        cp(B(z, 0, n), ps(1, 0, n), "s")
        if p == "n":
            tt(B(z, 96, 192), ps(0, 0, n), ab, A.add)
        tt(B("am" + p), ab, B("ml" if p == "n" else "mg", 0, n), A.mult)
        tt(B("sg" + p), ps(0, 0, n), B("am" + p), A.add if p == "n" else A.subtract)

    def parts_out(p, x, xlo):
        c0, n = (96, 224) if p == "o" else (0, 96)
        for b in range(4):
            mm(4 + b, max(n, 128), "eq", 128 * b, x, xlo)
        for b in range(4):
            cp(B("win", 4 * c0 + b, 4 * (c0 + n), 4), ps(4 + b, 0, n), "x")

    def turn(p, r):
        lo, hi = (384, 1280) if p == "o" else (0, 384)
        for s in range(1, 8):
            o = 1280 * s
            for d0, d1, s0 in ((0, 128 - 16 * s, 16 * s), (128 - 16 * s, 128, 0)):
                dma("y", "f%s%d" % (p, r), [("win", lo, hi, 1)], [("win", o + lo, o + hi, 1)], T.win[d0:d1, o + lo:o + hi], T.win[s0:s0 + d1 - d0, lo:hi], 14000.0 if p == "o" else 9000.0)

    turns = []

    def count(i, acc):
        n = 320 * (len(turns) % 4)
        turns.append(0)
        j = B("jk", n, n + width(i))

        def fn(e):
            if e is g.vector:
                return e.tensor_reduce(view(acc), view(i), AxisListType.X, A.add)
            return e.activation(view(j), view(i), ACT.Copy, accum_out=view(acc))
        op("x", [i], [j, acc], fn, 20 + acost(j, []))

    def compare_own():
        for k in range(14):
            own = B("soo", 16 * k + 15, 16 * k + 16)
            o = 896 * (k // 4) + k % 4
            for z, lo, hi, f in (("sgo", 16 * k, 16 * k + 16, A.is_lt), ("zzo", 16 * k + 16, 224, A.is_le)):
                if lo < hi:
                    ts(B("go", o + 4 * lo, o - k % 4 + 4 * hi, 4), B(z, lo, hi), own, f)
            if k < 13:
                count(B("go", o + 4 * (16 * k + 16), o - k % 4 + 896, 4), B("aft", k, k + 1))
        for q in range(4):
            lo = min(64 * q, 96)
            quant("gq", 224 * q + lo, 224 * q + 224, "go", 896 * q + 4 * lo)
            mm(3, 224, "cc", 0, "gq", 224 * q, q == 0, False)

    def compare_new():
        for k in range(6):
            own = B("son", 16 * k + 15, 16 * k + 16)
            q, t = divmod(k, 4)
            o = 1280 * q
            ts(B("gn", o + t, o + 896, 4), B("zzo"), own, A.is_gt)
            ts(B("gn", o + 896 + t, o + 1216, 4), B("zzn", 16 * k + 16, 96 + 16 * k), own, A.is_gt)
            ts(B("gn", o + 1216 + t, o + 1280, 4), B("sgn", 16 * k, 16 * k + 16), own, A.is_gt)
            count(B("gn", o + t, o + 1280, 4), B("acl", k, k + 1))
        for q in range(2):
            quant("gw", 224 * q, 224 * q + 224, "gn", 1280 * q)
            mm(3, 224, "cc", 128, "gw", 224 * q, False, q == 1)

    def early(r):
        x = "qt%d" % r
        products("o", x, 96)
        calls("o")
        scores("o")
        parts_out("o", x, 96)
        turn("o", r)
        compare_own()
        rows_own()

    def late(r, x):
        products("n", x, 0)
        calls("n")
        scores("n")
        parts_out("n", x, 0)
        turn("n", r)
        compare_new()
        cp(B("rk16", 0, 6), B("acl"))
        tt(B("rkc"), B("aft"), B("cs"), A.add)
        latch(B("cl"), ps(3, 0, 224))
        tt(B("rko"), B("cl", 15, 224, 16), B("rkc"), A.subtract)
        cp(B("rk16", 6, 20), B("rko"))
        op("v", [B("rk16"), B("sd")], [B("ob")], lambda e: e.tensor_copy(view(B("ob")).indirect(view(B("rk16"))), view(B("sd"))), 50 + 3.3 * CY * 320)
        latch(B("ol"), B("ob"))
        cp(B("ow", 0, 20), B("ol", 15, 320, 16))
        for s in range(1, 8):
            for d0, d1, s0 in ((0, 128 - 16 * s, 16 * s), (128 - 16 * s, 128, 0)):
                dma("y" if s % 2 else "s", "od%d" % r, [B("ow", 0, 20)], [B("ow", 20 * s, 20 * s + 20)], T.ow[d0:d1, 20 * s:20 * s + 20], T.ow[s0:s0 + d1 - d0, 0:20], 3500.0)
        rows_new()
        tt(B("os1"), ("@", B("ow"), B("rx")), B("ro4"), A.add)
        latch(B("os2"), B("os1"))
        for b in range(4):
            ts(B("fl%d" % b), B("os2", 15, 320, 16), cf(40 + b), A.add)
        t = "qt%d" % (r + 1)
        for (l0, l1) in ((0, 8), (8, 20)):
            for b in range(4):
                cp(B("tb", 64 * l0 + b, 64 * l1, 4), ("@", B("win"), B("fl%d" % b, l0, l1)), "x")
            quant(t, 16 * l0, 16 * l1, "tb", 64 * l0)
            if l0 == 0:
                send(r + 1)

    def send(r):
        t = "qt%d" % r
        dst = T.cores[(rank + r) % len(T.cores)]
        rid, pid = topo.addr(dst)[:2]
        m = topo.mask(core, dst)

        def fn():
            K["need"]("g", [B(t + "c", 0, 96), B(t + "s", 0, 96)], [], "ls", True)
            for k in "cs":
                o, i = T["ld%d%s" % (r, k)][:, 0:96], T[t + k][:, 0:96]
                if k == "c":
                    o, i = o.bitcast(dt.uint8), i.bitcast(dt.uint8)
                g.remote_dma(o, i, T.sem["rc%d" % r], T.sem["ls"], pid, rid, m)
                K["total"]["ls"] = K["total"].get("ls", 0) + len(topo.engines(core, dst))
        raw("g", [B(t + "c", 0, 96), B(t + "s", 0, 96)], [("sent%d" % r, 0, 1, 1)], fn, 600.0, 2000.0)

    def arrive(r):
        frm = T.cores[(rank - r) % len(T.cores)]
        n = 2 * len(topo.engines(frm, core))
        raw("t", [("sent%d" % r, 0, 1, 1)], [B("ld%dc" % r, 0, 96), B("ld%ds" % r, 0, 96)], lambda: K["wait"]("t", "rc%d" % r, n, {}), 1.0, 0.0)
        for b in range(4):
            a = (0, 1, 2, 0)[b]
            mm(4 + b, 128, "wq", 128 * b, "ld%d" % r, 0)
            mm(a, 128, "eq", 128 * b, "ld%d" % r, 0)
            o, i = B("rl", 96 * b, 96 * b + 96), ps(4 + b, 0, 96)
            op("s", [i], [o], lambda e, o=o, i=i: e.activation(view(o), view(i), ACT.Relu, scale=0.03125), acost(o, []))
            tt(B("xnb", b, 384, 4), o, ps(a, 0, 96), A.add)
        quant("xn%d" % r, 0, 128, "xnb", 0)

    early(0)
    late(0, "qt0")
    for r in (1, 2):
        early(r)
        arrive(r)
        late(r, "xn%d" % r)
    x = "qt3"
    mm(3, 224, "vq", 0, x, 96)
    cp(B("yb", 96, 320), ps(3, 0, 224), "s")
    ts(B("rwa"), B("row"), 0.05, A.mult, G_, A.add)
    cp(B("rwi"), B("rwa"))
    ts(B("rwa"), B("rwi"), 7.5, A.is_ge, -8.0, A.mult)
    tt(B("rwb"), B("rwa"), B("rwi"), A.add)
    dma("y", "out", [B(x + "c", 96, 320)], [], T.oc[:, 384:1280], T[x + "c"][:, 96:320].bitcast(dt.uint8))
    for k in range(4):
        dma("y", "out", [B(x + "s", 96, 320)], [], T.osc[4 * k:4 * k + 4, 96:320], T[x + "s"][32 * k:32 * k + 4, 96:320])
    dma("y", "out", [B("yb", 96, 320)], [], T.y[:, 96:320], T.yb[:, 96:320])
    dma("s", "out", [B("rwb")], [], T.rw[:, :], T.rwb[0:128:16, :])
    arrive(3)
    x = "xn3"
    mm(3, 128, "vq", 0, x, 0)
    cp(B("yb", 0, 96), ps(3, 0, 96), "s")
    dma("s", "out", [B(x + "c", 0, 96)], [], T.oc[:, 0:384], T[x + "c"][:, 0:96].bitcast(dt.uint8))
    for k in range(4):
        dma("s" if k % 2 else "y", "out", [B(x + "s", 0, 96)], [], T.osc[4 * k:4 * k + 4, 0:96], T[x + "s"][32 * k:32 * k + 4, 0:96])
    dma("y", "out", [B("yb", 0, 96)], [], T.y[:, 0:96], T.yb[:, 0:96])
    K["run"]()
    for sem, n in sorted(K["total"].items()):
        K["wait"]("g", sem, n, {})
